import numpy as np
import ml_dtypes


def mxq(x, axis, fmt="e4m3"):
    dtype, down = {"e4m3": (ml_dtypes.float8_e4m3fn, 7), "e5m2": (ml_dtypes.float8_e5m2, 14)}[fmt]
    v = np.moveaxis(np.asarray(x, np.float32).astype(ml_dtypes.bfloat16).astype(np.float64), axis, -1)
    blocks = v.reshape(v.shape[:-1] + (-1, 32))
    amax = np.abs(blocks).max(-1, keepdims=True)
    byte = np.maximum(np.where(amax > 0, np.frexp(amax)[1] - 1 + 127, 0) - down, 1)
    scale = np.exp2(byte - 127.0)
    codes = (blocks / scale).astype(np.float32).astype(dtype).astype(np.float64)
    return np.moveaxis((codes * scale).reshape(v.shape), -1, axis)


WIDE = False


def mx_kscale(k):
    if not WIDE:
        return np.ones(k)
    levels = np.array([10, -10, 5, -5, 0])
    if k % 512:
        return np.exp2(np.random.permutation(np.resize(levels, k // 32))).repeat(32)
    a = np.empty((k // 512, 16))
    for p in range(k // 512):
        a[p, :8] = np.random.permutation(np.resize(levels, 8))
        for g in range(8):
            far = levels[np.abs(levels - a[p, g]) >= 10]
            a[p, g + 8] = far[np.random.randint(len(far))]
    return np.exp2(a.ravel()).repeat(32)


BF16 = ml_dtypes.bfloat16


def bf(x):
    return np.asarray(x, np.float32).astype(BF16)


def f64(x):
    return np.asarray(x).astype(np.float64)


E2M1 = np.array([0.0, 0.5, 1.0, 1.5, 2.0, 3.0, 4.0, 6.0, -0.0, -0.5, -1.0, -1.5, -2.0, -3.0, -4.0, -6.0])


def pack_weight(w, fmt):
    k, n = w.shape
    w = f64(bf(w)).reshape(k // 32, 32, n)
    amax = np.abs(w).max(1)
    if fmt == "e4m3":
        byte = np.frexp(amax)[1] - 1 + 127 - 7
    else:
        mant, ex = np.frexp(amax / 6.0)
        byte = np.where(mant > 0.5, ex, ex - 1) + 127
    byte = np.clip(np.where(amax > 0, byte, 1), 1, 254)
    scaled = (w * np.exp2(127.0 - byte)[:, None, :]).reshape(k, n).astype(np.float32)
    by_word = np.ascontiguousarray(scaled.reshape(k // 512, 128, 4, n).transpose(0, 1, 3, 2))
    if fmt == "e4m3":
        words = by_word.astype(ml_dtypes.float8_e4m3fn).view(np.uint8)
    else:
        c = by_word.astype(ml_dtypes.float4_e2m1fn).view(np.uint8) & 0xF
        words = c[..., 0::2] | (c[..., 1::2] << 4)
    return np.ascontiguousarray(words), np.ascontiguousarray(byte.astype(np.uint8).reshape(k // 512, 16, n))


def unpack_weight(words, scales, fmt):
    g, p, n, _ = words.shape
    if fmt == "e4m3":
        vals = np.ascontiguousarray(words).view(ml_dtypes.float8_e4m3fn).astype(np.float64)
    else:
        nib = np.empty((g, p, n, 4), np.uint8)
        nib[..., 0::2] = words & 0xF
        nib[..., 1::2] = words >> 4
        vals = E2M1[nib]
    vals = vals * np.repeat(np.exp2(scales.astype(np.float64) - 127.0), 8, axis=1)[..., None]
    return vals.transpose(0, 1, 3, 2).reshape(g * 512, n)
def pack4(w):
    words, scales = pack_weight(w, "e2m1")
    return words.reshape(words.shape[0], 128, -1), scales


def unpack4(words, scales):
    return unpack_weight(words.reshape(words.shape[0], 128, -1, 2), scales, "e2m1")


V, K, T = 2560, 1024, 512


def setup_inputs():
    s = mx_kscale(K)
    phi = np.random.standard_normal((V, K)) * np.exp(0.2 * np.random.standard_normal((V, 1)))
    c = np.exp(0.3 * np.random.standard_normal(K)) * s
    lam = 2 * np.cumsum(np.random.random(K)) / K
    tau = 2 * 8 ** (np.arange(T) / (T - 1))
    heat = np.exp(-lam[:, None] * tau)
    heat = heat / heat.sum(axis=0)
    gate = np.random.standard_normal((K, T)) / np.sqrt(K)
    resp = np.random.standard_normal((K, T)) / np.sqrt(K)
    gate_words, gate_scales = pack4(gate / s[:, None])
    resp_words, resp_scales = pack_weight(resp / s[:, None], "e4m3")
    return {"phi": bf(phi),
            "c": bf(c),
            "heat": bf(heat / s[:, None]),
            "gate_words": gate_words, "gate_scales": gate_scales,
            "resp_words": resp_words, "resp_scales": resp_scales,
            "bias": bf(0.4 * np.random.standard_normal(T))}


def reference(phi, c, heat, gate_words, gate_scales, resp_words, resp_scales, bias):
    a = mxq(np.square(f64(phi)) * f64(c), 1, "e4m3")
    h = a @ mxq(f64(heat), 0, "e4m3")
    z = a @ unpack4(gate_words, gate_scales)
    d = a @ unpack_weight(resp_words, resp_scales, "e4m3")
    gate = 1 / (1 + np.exp(-(z + f64(bias))))
    return h * gate + d

@@ -1,0 +1,292 @@
+from contextlib import ExitStack
+
+import concourse.mybir as mybir
+from concourse.masks import make_identity
+
+V, K, T = 2560, 1024, 512
+FLOPS = 3 * 2 * V * K * T
+
+F32 = mybir.dt.float32
+BF16 = mybir.dt.bfloat16
+I32 = mybir.dt.int32
+U32 = mybir.dt.uint32
+U8 = mybir.dt.uint8
+FP8X4 = mybir.dt.float8_e4m3fn_x4
+FP4X4 = mybir.dt.float4_e2m1fn_x4
+ACT = mybir.ActivationFunctionType
+ALU = mybir.AluOpType
+
+P = 128
+PACK = 4
+PASSES = K // (P * PACK)
+TILES = V // P
+PAIR = 2 * P
+PAIRS = V // PAIR
+POOL_COLS = 384
+POOL_STEP = 256
+WB = 1
+H0 = 256
+HW = 0
+LO = 0
+Q1 = 0
+H2 = 384
+QE = 1
+TP = 0
+
+
+def tile_gated_heat_signature_s10_kernel(
+    tc, phi, c, heat, gate_words, gate_scales, resp_words, resp_scales, bias, out
+):
+    nc = tc.nc
+    with ExitStack() as ctx:
+        keep = ctx.enter_context(tc.tile_pool(name="keep", bufs=1))
+        work = ctx.enter_context(tc.tile_pool(name="work", bufs=3))
+        psum = ctx.enter_context(tc.psum_pool(name="psum", bufs=2))
+        ctx.enter_context(tc.manual_schedule())
+
+        ident = keep.tile([P, P], F32, name="ident")
+        c_bf = keep.tile([P, PASSES, PACK], BF16, name="c_bf")
+        c_f = keep.tile([P, P], F32, name="c_f")
+        c_rows = keep.tile([P, P], F32, name="c_rows")
+        c_ps = psum.tile([P, 2, P], F32, name="c_ps", bufs=1)
+        bias_bf = keep.tile([P, PACK], BF16, name="bias_bf")
+        bias_f = keep.tile([P, PACK], F32, name="bias_f")
+        bias_row = keep.tile([P, T], F32, name="bias_row")
+        warm_in = keep.tile([P, 1], F32, name="warm_in")
+        warm_out = keep.tile([P, 1], F32, name="warm_out")
+        gate_w = keep.tile([P, PASSES, 2 * T], U8, name="gate_w", align_bytes=64)
+        gate_s = keep.tile([P, PASSES, T], U8, name="gate_s", align_bytes=64)
+        resp_w = keep.tile([P, PASSES, T], U32, name="resp_w", align_bytes=64)
+        resp_s = keep.tile([P, PASSES, T], U8, name="resp_s", align_bytes=64)
+        heat_raw = [keep.tile([P, PACK, T], BF16, name="heat_raw%d" % g) for g in range(PASSES)]
+        heat_bf = [keep.tile([P, T, PACK], BF16, name="heat_bf%d" % g, align_bytes=64) for g in range(PASSES)]
+        heat_w = [keep.tile([P, T], U32, name="heat_w%d" % g, align_bytes=64) for g in range(PASSES)]
+        heat_s = [keep.tile([P, T], U8, name="heat_s%d" % g, align_bytes=64) for g in range(PASSES)]
+        phi_sb = [keep.tile([P, K], BF16, name="phi%d" % i) for i in range(TILES)]
+
+        turned, squares, weighted, codes, scales = {}, {}, {}, {}, {}
+        banks, logits, gates, gated = {}, {}, {}, {}
+
+        def load_phi(i):
+            nc.sync.dma_start(out=phi_sb[i][:], in_=phi[i * P : (i + 1) * P, :])
+
+        def load_heat(g):
+            rows = heat[g * P * PACK : (g + 1) * P * PACK, :]
+            nc.sync.dma_start(out=heat_raw[g][:], in_=rows.rearrange("(p j) n -> p j n", j=PACK))
+
+        def load_scales(plane, src):
+            for q in range(4):
+                nc.sync.dma_start(
+                    out=plane[32 * q : 32 * q + 4, :, :].bitcast(I32),
+                    in_=src[:, 4 * q : 4 * q + 4, :].rearrange("g r n -> r g n").bitcast(I32),
+                )
+
+        def weave_heat(g):
+            nc.vector.tensor_copy(
+                out=heat_bf[g][:].rearrange("p (n i) t -> p n t i", i=4),
+                in_=heat_raw[g][:].rearrange("p t (n i) -> p n t i", i=4),
+            )
+
+        def quantize_heat(g):
+            nc.vector.quantize_mx(
+                out=heat_w[g][:].bitcast(FP8X4),
+                scales=heat_s[g][:],
+                in_=heat_bf[g][:].rearrange("p n t -> p (n t)"),
+            )
+
+        def weave_heat_scalar(g):
+            nc.scalar.copy(
+                out=heat_bf[g][:].rearrange("p (n i) t -> p n t i", i=4),
+                in_=heat_raw[g][:].rearrange("p t (n i) -> p n t i", i=4),
+            )
+
+        def weave_heat_pool(g):
+            for n0 in range(0, T, P):
+                nc.gpsimd.tensor_scalar(
+                    out=heat_bf[g][:, n0 : n0 + P, :],
+                    in0=heat_raw[g][:, :, n0 : n0 + P].rearrange("p t n -> p n t"),
+                    scalar1=1.0,
+                    scalar2=0.0,
+                    op0=ALU.mult,
+                    op1=ALU.add,
+                )
+
+        def turn(n, tag="turn", bufs=2):
+            for g in range(PASSES):
+                bank = psum.tile([P, 2, PAIR], F32, name=tag, bufs=bufs)
+                turned[n, g] = bank
+                for j in range(2):
+                    words = phi_sb[2 * n + j][:].bitcast(F32)
+                    for u in range(2):
+                        nc.tensor.transpose(
+                            bank[:, u, j * P : (j + 1) * P], words[:, 256 * g + u : 256 * (g + 1) : 2], ident[:]
+                        )
+
+        def square(n, g):
+            sq = work.tile([P, PAIR, PACK], F32, name="sq", bufs=4)
+            squares[n, g] = sq
+            nc.scalar.activation(
+                out=sq[:].rearrange("p v (u e) -> p v u e", e=2),
+                in_=turned[n, g][:].bitcast(BF16).rearrange("p u (v e) -> p v u e", e=2),
+                func=ACT.Square,
+            )
+
+        def weigh(n, lo, hi, engine, factor):
+            if n not in weighted:
+                weighted[n] = work.tile([P, PASSES, PAIR, PACK], BF16, name="weighted", align_bytes=64, bufs=WB)
+            for g in range(PASSES):
+                a, b = max(lo - g * PAIR, 0), min(hi - g * PAIR, PAIR)
+                if a < b:
+                    engine.tensor_tensor(
+                        out=weighted[n][:, g, a:b, :],
+                        in0=squares[n, g][:, a:b, :],
+                        in1=factor[:, g * PACK : (g + 1) * PACK].unsqueeze(1).to_broadcast([P, b - a, PACK]),
+                        op=ALU.mult,
+                    )
+
+        def weigh_pool(n, hi):
+            for lo in range(0, hi, POOL_STEP):
+                weigh(n, lo, min(lo + POOL_STEP, hi), nc.gpsimd, c_f)
+
+        def weigh_vector(n, lo, hi):
+            weigh(n, lo, hi, nc.vector, c_ps[:, 1, :])
+
+        def quantize(n, g0, g1):
+            if n not in codes:
+                codes[n] = work.tile([P, PASSES, PAIR], U32, name="codes", align_bytes=64, bufs=4)
+                scales[n] = work.tile([P, PASSES, PAIR], U8, name="scales", align_bytes=64, bufs=4)
+            nc.vector.quantize_mx(
+                out=codes[n][:, g0:g1, :].rearrange("p g v -> p (g v)").bitcast(FP8X4),
+                scales=scales[n][:, g0:g1, :].rearrange("p g v -> p (g v)"),
+                in_=weighted[n][:, g0:g1, :, :].rearrange("p g v t -> p (g v t)"),
+            )
+
+        def product(i, kind):
+            bank = psum.tile([P, T], F32, name="acc", bufs=5)
+            banks[i, kind] = bank
+            n, cols = i // 2, slice((i % 2) * P, (i % 2 + 1) * P)
+            for g in range(PASSES):
+                rhs, rhs_scale = {
+                    "z": (gate_w[:, g, :].bitcast(FP4X4), gate_s[:, g, :]),
+                    "h": (heat_w[g][:].bitcast(FP8X4), heat_s[g][:]),
+                    "d": (resp_w[:, g, :].bitcast(FP8X4), resp_s[:, g, :]),
+                }[kind]
+                nc.tensor.matmul_mx(
+                    out=bank[:],
+                    lhsT=codes[n][:, g, cols].bitcast(FP8X4),
+                    lhsT_scale=scales[n][:, g, cols],
+                    rhs=rhs,
+                    rhs_scale=rhs_scale,
+                    start=(g == 0),
+                    stop=(g == PASSES - 1),
+                )
+
+        def add_bias(i):
+            logits[i] = work.tile([P, T], F32, name="logits")
+            nc.vector.tensor_tensor(out=logits[i][:], in0=banks[i, "z"][:], in1=bias_row[:], op=ALU.add)
+
+        def sigmoid(i):
+            gates[i] = work.tile([P, T], F32, name="gates", bufs=4)
+            nc.scalar.activation(out=gates[i][:], in_=logits[i][:], func=ACT.Sigmoid)
+
+        def apply_gate(i):
+            gated[i] = work.tile([P, T], F32, name="gated")
+            nc.vector.tensor_tensor(out=gated[i][:], in0=banks[i, "h"][:], in1=gates[i][:], op=ALU.mult)
+
+        def finish(i):
+            result = work.tile([P, T], F32, name="result", bufs=4)
+            nc.vector.tensor_tensor(out=result[:], in0=banks[i, "d"][:], in1=gated[i][:], op=ALU.add)
+            nc.sync.dma_start(out=out[i * P : (i + 1) * P, :], in_=result[:])
+
+        nc.vector.memset(c_f[:], 0.0)
+        nc.vector.memset(warm_in[:], 0.0)
+        nc.vector.memset(gate_s[:].bitcast(I32), 0)
+        nc.vector.memset(resp_s[:].bitcast(I32), 0)
+        nc.scalar.activation(out=warm_out[:], in_=warm_in[:], func=ACT.Sigmoid)
+        make_identity(nc, ident[:])
+
+        nc.sync.dma_start(out=c_bf[:], in_=c.rearrange("(g p t) -> p g t", g=PASSES, t=PACK))
+        nc.sync.dma_start(out=bias_bf[:], in_=bias.rearrange("(p j) -> p j", j=PACK))
+        if LO == 0:
+            load_heat(0)
+        load_phi(0)
+        load_phi(1)
+        if LO == 1:
+            load_heat(0)
+        load_heat(1)
+        load_phi(2)
+        load_phi(3)
+        nc.sync.dma_start(out=gate_w[:].bitcast(I32), in_=gate_words.rearrange("g p n -> p g n").bitcast(I32))
+        load_scales(gate_s, gate_scales)
+        load_phi(4)
+        load_phi(5)
+        load_scales(resp_s, resp_scales)
+        nc.sync.dma_start(out=resp_w[:].bitcast(I32), in_=resp_words.rearrange("g p n t -> p g (n t)").bitcast(I32))
+        for i in range(6, TILES):
+            load_phi(i)
+
+        nc.vector.tensor_copy(out=c_f[:, : PASSES * PACK], in_=c_bf[:].rearrange("p g t -> p (g t)"))
+        nc.vector.tensor_copy(out=bias_f[:], in_=bias_bf[:])
+        nc.tensor.transpose(c_ps[:, 0, :], c_f[:], ident[:])
+        nc.scalar.copy(out=c_rows[:], in_=c_ps[:, 0, :])
+        spread = psum.tile([P, PACK, P], F32, name="acc", bufs=5)
+        if LO == 0:
+            for j in range(PACK):
+                nc.tensor.transpose(spread[:, j, :], bias_f[:, j : j + 1].to_broadcast([P, P]), ident[:])
+            nc.scalar.copy(out=bias_row[:].rearrange("p (n j) -> p n j", j=PACK), in_=spread[:].rearrange("p j n -> p n j"))
+        weave_heat(0)
+        turn(0)
+        nc.tensor.transpose(c_ps[:, 1, :], c_rows[:], ident[:])
+        square(0, 0)
+        square(0, 1)
+        quantize_heat(0)
+        weave_heat_pool(1)
+        if LO == 1:
+            for j in range(PACK):
+                nc.tensor.transpose(spread[:, j, :], bias_f[:, j : j + 1].to_broadcast([P, P]), ident[:])
+        turn(1, "acc", 5)
+        square(1, 0)
+        square(1, 1)
+        if LO == 1:
+            nc.scalar.copy(out=bias_row[:].rearrange("p (n j) -> p n j", j=PACK), in_=spread[:].rearrange("p j n -> p n j"))
+        weigh_vector(0, 0, PAIR)
+        weigh_vector(0, PAIR, 2 * PAIR)
+        quantize(0, 0, 2)
+        quantize_heat(1)
+        weigh_pool(1, H0)
+        turn(2)
+        square(2, 0)
+        product(0, "z")
+        weigh_vector(1, H0, 2 * PAIR)
+        add_bias(0)
+        sigmoid(0)
+        square(2, 1)
+        if Q1 == 0:
+            quantize(1, 0, 2)
+            weigh_pool(2, POOL_COLS)
+
+        for n in range(PAIRS):
+            for i in (2 * n, 2 * n + 1):
+                product(i, "h")
+                apply_gate(i)
+                if i + 1 < TILES:
+                    product(i + 1, "z")
+                    add_bias(i + 1)
+                    sigmoid(i + 1)
+                product(i, "d")
+                finish(i)
+                if i % 2 == 0:
+                    if i == 0 and Q1:
+                        quantize(1, 0, 2)
+                        weigh_pool(2, H2)
+                    if n + 2 < PAIRS:
+                        weigh_vector(n + 2, H2 if i == 0 else POOL_COLS, 2 * PAIR)
+                    if n + 3 < PAIRS:
+                        turn(n + 3)
+                        square(n + 3, 0)
+                else:
+                    if n + 2 < PAIRS:
+                        quantize(n + 2, 0, 2)
+                    if n + 3 < PAIRS:
+                        square(n + 3, 1)
+                        weigh_pool(n + 3, POOL_COLS)

@@ -22,16 +22,21 @@ PASSES = K // (P * PACK)
 TILES = V // P
 PAIR = 2 * P
 PAIRS = V // PAIR
-POOL_COLS = 384
-POOL_STEP = 256
+POOL_COLS = 176
 WB = 1
-H0 = 256
-HW = 0
-LO = 0
-Q1 = 0
-H2 = 384
+S1 = 128
+S2 = 176
+W0 = "g"
+W1 = "a"
+TAILG = 1
+ZE = 1
+LO = "0a1b23g45r"
+BR = 0
+TE = 0
 QE = 1
-TP = 0
+TL = 2
+WP = 2
+SORT = 0
 
 
 def tile_gated_heat_signature_s10_kernel(
@@ -65,7 +70,7 @@ def tile_gated_heat_signature_s10_kernel(
         phi_sb = [keep.tile([P, K], BF16, name="phi%d" % i) for i in range(TILES)]
 
         turned, squares, weighted, codes, scales = {}, {}, {}, {}, {}
-        banks, logits, gates, gated = {}, {}, {}, {}
+        banks, logits, gates, gated, parted = {}, {}, {}, {}, {}
 
         def load_phi(i):
             nc.sync.dma_start(out=phi_sb[i][:], in_=phi[i * P : (i + 1) * P, :])
@@ -111,60 +116,67 @@ def tile_gated_heat_signature_s10_kernel(
                     op1=ALU.add,
                 )
 
-        def turn(n, tag="turn", bufs=2):
+        def turn(i, tag="turn", bufs=2):
+            bank = psum.tile([P, PASSES, 2, P], F32, name=tag, bufs=bufs)
+            turned[i] = bank
+            words = phi_sb[i][:].bitcast(F32)
             for g in range(PASSES):
-                bank = psum.tile([P, 2, PAIR], F32, name=tag, bufs=bufs)
-                turned[n, g] = bank
-                for j in range(2):
-                    words = phi_sb[2 * n + j][:].bitcast(F32)
-                    for u in range(2):
-                        nc.tensor.transpose(
-                            bank[:, u, j * P : (j + 1) * P], words[:, 256 * g + u : 256 * (g + 1) : 2], ident[:]
-                        )
+                for u in range(2):
+                    if (i, g) in parted:
+                        nc.tensor.transpose(bank[:, g, u, :], parted[i, g][:, u, :], ident[:])
+                    else:
+                        nc.tensor.transpose(bank[:, g, u, :], words[:, 256 * g + u : 256 * (g + 1) : 2], ident[:])
 
-        def square(n, g):
-            sq = work.tile([P, PAIR, PACK], F32, name="sq", bufs=4)
-            squares[n, g] = sq
+        def part(i, g):
+            parted[i, g] = work.tile([P, 2, P], F32, name="parted", bufs=4)
+            words = phi_sb[i][:].bitcast(F32)
+            nc.scalar.copy(out=parted[i, g][:], in_=words[:, 256 * g : 256 * (g + 1)].rearrange("p (q u) -> p u q", u=2))
+
+        def square(i):
+            sq = work.tile([P, P, PASSES * PACK], F32, name="sq", bufs=4)
+            squares[i] = sq
             nc.scalar.activation(
-                out=sq[:].rearrange("p v (u e) -> p v u e", e=2),
-                in_=turned[n, g][:].bitcast(BF16).rearrange("p u (v e) -> p v u e", e=2),
+                out=sq[:].rearrange("p v (w e) -> p v w e", e=2),
+                in_=turned[i][:].bitcast(BF16).rearrange("p g u (v e) -> p v (g u) e", e=2),
                 func=ACT.Square,
             )
 
         def weigh(n, lo, hi, engine, factor):
             if n not in weighted:
-                weighted[n] = work.tile([P, PASSES, PAIR, PACK], BF16, name="weighted", align_bytes=64, bufs=WB)
-            for g in range(PASSES):
-                a, b = max(lo - g * PAIR, 0), min(hi - g * PAIR, PAIR)
+                weighted[n] = work.tile([P, 2, PASSES, P, PACK], BF16, name="weighted", align_bytes=64, bufs=WB)
+            for j in range(2):
+                a, b = max(lo - j * P, 0), min(hi - j * P, P)
                 if a < b:
                     engine.tensor_tensor(
-                        out=weighted[n][:, g, a:b, :],
-                        in0=squares[n, g][:, a:b, :],
-                        in1=factor[:, g * PACK : (g + 1) * PACK].unsqueeze(1).to_broadcast([P, b - a, PACK]),
+                        out=weighted[n][:, j, :, a:b, :],
+                        in0=squares[2 * n + j][:, a:b, :].rearrange("p v (g t) -> p g v t", t=PACK),
+                        in1=factor[:, : PASSES * PACK]
+                        .rearrange("p (g t) -> p g t", t=PACK)
+                        .unsqueeze(2)
+                        .to_broadcast([P, PASSES, b - a, PACK]),
                         op=ALU.mult,
                     )
 
         def weigh_pool(n, hi):
-            for lo in range(0, hi, POOL_STEP):
-                weigh(n, lo, min(lo + POOL_STEP, hi), nc.gpsimd, c_f)
+            weigh(n, 0, hi, nc.gpsimd, c_f)
 
         def weigh_vector(n, lo, hi):
             weigh(n, lo, hi, nc.vector, c_ps[:, 1, :])
 
-        def quantize(n, g0, g1):
+        def quantize(n, j0, j1):
             if n not in codes:
-                codes[n] = work.tile([P, PASSES, PAIR], U32, name="codes", align_bytes=64, bufs=4)
-                scales[n] = work.tile([P, PASSES, PAIR], U8, name="scales", align_bytes=64, bufs=4)
+                codes[n] = work.tile([P, 2, PASSES, P], U32, name="codes", align_bytes=64, bufs=4)
+                scales[n] = work.tile([P, 2, PASSES, P], U8, name="scales", align_bytes=64, bufs=4)
             nc.vector.quantize_mx(
-                out=codes[n][:, g0:g1, :].rearrange("p g v -> p (g v)").bitcast(FP8X4),
-                scales=scales[n][:, g0:g1, :].rearrange("p g v -> p (g v)"),
-                in_=weighted[n][:, g0:g1, :, :].rearrange("p g v t -> p (g v t)"),
+                out=codes[n][:, j0:j1, :, :].rearrange("p j g v -> p (j g v)").bitcast(FP8X4),
+                scales=scales[n][:, j0:j1, :, :].rearrange("p j g v -> p (j g v)"),
+                in_=weighted[n][:, j0:j1, :, :, :].rearrange("p j g v t -> p (j g v t)"),
             )
 
         def product(i, kind):
             bank = psum.tile([P, T], F32, name="acc", bufs=5)
             banks[i, kind] = bank
-            n, cols = i // 2, slice((i % 2) * P, (i % 2 + 1) * P)
+            n, j = divmod(i, 2)
             for g in range(PASSES):
                 rhs, rhs_scale = {
                     "z": (gate_w[:, g, :].bitcast(FP4X4), gate_s[:, g, :]),
@@ -173,8 +185,8 @@ def tile_gated_heat_signature_s10_kernel(
                 }[kind]
                 nc.tensor.matmul_mx(
                     out=bank[:],
-                    lhsT=codes[n][:, g, cols].bitcast(FP8X4),
-                    lhsT_scale=scales[n][:, g, cols],
+                    lhsT=codes[n][:, j, g, :].bitcast(FP8X4),
+                    lhsT_scale=scales[n][:, j, g, :],
                     rhs=rhs,
                     rhs_scale=rhs_scale,
                     start=(g == 0),
@@ -186,7 +198,7 @@ def tile_gated_heat_signature_s10_kernel(
             nc.vector.tensor_tensor(out=logits[i][:], in0=banks[i, "z"][:], in1=bias_row[:], op=ALU.add)
 
         def sigmoid(i):
-            gates[i] = work.tile([P, T], F32, name="gates", bufs=4)
+            gates[i] = work.tile([P, T], F32, name="gates", bufs=5)
             nc.scalar.activation(out=gates[i][:], in_=logits[i][:], func=ACT.Sigmoid)
 
         def apply_gate(i):
@@ -195,33 +207,43 @@ def tile_gated_heat_signature_s10_kernel(
 
         def finish(i):
             result = work.tile([P, T], F32, name="result", bufs=4)
-            nc.vector.tensor_tensor(out=result[:], in0=banks[i, "d"][:], in1=gated[i][:], op=ALU.add)
+            if TILES - TL - TAILG <= i < TILES - TL:
+                resp = work.tile([P, T], F32, name="resp")
+                nc.scalar.copy(out=resp[:], in_=banks[i, "d"][:])
+                nc.gpsimd.tensor_tensor(out=result[:], in0=resp[:], in1=gated[i][:], op=ALU.add)
+            else:
+                nc.vector.tensor_tensor(out=result[:], in0=banks[i, "d"][:], in1=gated[i][:], op=ALU.add)
             nc.sync.dma_start(out=out[i * P : (i + 1) * P, :], in_=result[:])
 
-        nc.vector.memset(c_f[:], 0.0)
-        nc.vector.memset(warm_in[:], 0.0)
+        def gate_logits(i):
+            product(i, "z")
+            add_bias(i)
+            sigmoid(i)
+
+        weavers = {"g": weave_heat_pool, "v": weave_heat, "a": weave_heat_scalar}
+
         nc.vector.memset(gate_s[:].bitcast(I32), 0)
+        nc.vector.memset(warm_in[:], 0.0)
+        nc.vector.memset(c_f[:], 0.0)
         nc.vector.memset(resp_s[:].bitcast(I32), 0)
         nc.scalar.activation(out=warm_out[:], in_=warm_in[:], func=ACT.Sigmoid)
         make_identity(nc, ident[:])
 
         nc.sync.dma_start(out=c_bf[:], in_=c.rearrange("(g p t) -> p g t", g=PASSES, t=PACK))
         nc.sync.dma_start(out=bias_bf[:], in_=bias.rearrange("(p j) -> p j", j=PACK))
-        if LO == 0:
-            load_heat(0)
-        load_phi(0)
-        load_phi(1)
-        if LO == 1:
-            load_heat(0)
-        load_heat(1)
-        load_phi(2)
-        load_phi(3)
-        nc.sync.dma_start(out=gate_w[:].bitcast(I32), in_=gate_words.rearrange("g p n -> p g n").bitcast(I32))
-        load_scales(gate_s, gate_scales)
-        load_phi(4)
-        load_phi(5)
-        load_scales(resp_s, resp_scales)
-        nc.sync.dma_start(out=resp_w[:].bitcast(I32), in_=resp_words.rearrange("g p n t -> p g (n t)").bitcast(I32))
+        for what in LO:
+            if what == "a":
+                load_heat(0)
+            elif what == "b":
+                load_heat(1)
+            elif what == "g":
+                nc.sync.dma_start(out=gate_w[:].bitcast(I32), in_=gate_words.rearrange("g p n -> p g n").bitcast(I32))
+                load_scales(gate_s, gate_scales)
+            elif what == "r":
+                load_scales(resp_s, resp_scales)
+                nc.sync.dma_start(out=resp_w[:].bitcast(I32), in_=resp_words.rearrange("g p n t -> p g (n t)").bitcast(I32))
+            else:
+                load_phi(int(what))
         for i in range(6, TILES):
             load_phi(i)
 
@@ -230,63 +252,87 @@ def tile_gated_heat_signature_s10_kernel(
         nc.tensor.transpose(c_ps[:, 0, :], c_f[:], ident[:])
         nc.scalar.copy(out=c_rows[:], in_=c_ps[:, 0, :])
         spread = psum.tile([P, PACK, P], F32, name="acc", bufs=5)
-        if LO == 0:
-            for j in range(PACK):
-                nc.tensor.transpose(spread[:, j, :], bias_f[:, j : j + 1].to_broadcast([P, P]), ident[:])
-            nc.scalar.copy(out=bias_row[:].rearrange("p (n j) -> p n j", j=PACK), in_=spread[:].rearrange("p j n -> p n j"))
-        weave_heat(0)
         turn(0)
+        square(0)
         nc.tensor.transpose(c_ps[:, 1, :], c_rows[:], ident[:])
-        square(0, 0)
-        square(0, 1)
-        quantize_heat(0)
-        weave_heat_pool(1)
-        if LO == 1:
-            for j in range(PACK):
-                nc.tensor.transpose(spread[:, j, :], bias_f[:, j : j + 1].to_broadcast([P, P]), ident[:])
-        turn(1, "acc", 5)
-        square(1, 0)
-        square(1, 1)
-        if LO == 1:
+        for j in range(PACK):
+            nc.tensor.transpose(spread[:, j, :], bias_f[:, j : j + 1].to_broadcast([P, P]), ident[:])
+        if BR == 0:
             nc.scalar.copy(out=bias_row[:].rearrange("p (n j) -> p n j", j=PACK), in_=spread[:].rearrange("p j n -> p n j"))
-        weigh_vector(0, 0, PAIR)
-        weigh_vector(0, PAIR, 2 * PAIR)
+        turn(1)
+        square(1)
+        weave_heat(0)
+        weigh_vector(0, 0, P)
+        quantize_heat(0)
+        if WP == 0:
+            weavers[W1](1)
+        turn(2, "acc", 5)
+        turn(3, "acc", 5)
+        square(2)
+        if WP == 1:
+            weavers[W1](1)
+        square(3)
+        if WP == 2:
+            weavers[W1](1)
+        if BR == 1:
+            nc.scalar.copy(out=bias_row[:].rearrange("p (n j) -> p n j", j=PACK), in_=spread[:].rearrange("p j n -> p n j"))
+        weigh_vector(0, P, PAIR)
         quantize(0, 0, 2)
-        quantize_heat(1)
-        weigh_pool(1, H0)
-        turn(2)
-        square(2, 0)
+        if WP < 2:
+            quantize_heat(1)
+        weigh_pool(1, S1)
+        if TE:
+            turn(4)
+            turn(5)
         product(0, "z")
-        weigh_vector(1, H0, 2 * PAIR)
+        if not TE:
+            turn(4)
+            turn(5)
+        weigh_vector(1, S1, PAIR)
         add_bias(0)
+        if WP == 2:
+            quantize_heat(1)
+        square(4)
         sigmoid(0)
-        square(2, 1)
-        if Q1 == 0:
+        square(5)
+        if ZE == 2:
+            gate_logits(1)
+        if QE:
             quantize(1, 0, 2)
-            weigh_pool(2, POOL_COLS)
+            weigh_pool(2, S2)
 
+        done = ZE
         for n in range(PAIRS):
             for i in (2 * n, 2 * n + 1):
                 product(i, "h")
                 apply_gate(i)
-                if i + 1 < TILES:
-                    product(i + 1, "z")
-                    add_bias(i + 1)
-                    sigmoid(i + 1)
+                if done == i + 1 < TILES:
+                    gate_logits(done)
+                    done = done + 1
                 product(i, "d")
                 finish(i)
+                if i >= TILES - 4 and done < TILES:
+                    gate_logits(done)
+                    done = done + 1
                 if i % 2 == 0:
-                    if i == 0 and Q1:
+                    if i == 0 and not QE:
                         quantize(1, 0, 2)
-                        weigh_pool(2, H2)
+                        weigh_pool(2, S2)
                     if n + 2 < PAIRS:
-                        weigh_vector(n + 2, H2 if i == 0 else POOL_COLS, 2 * PAIR)
+                        weigh_vector(n + 2, S2 if i == 0 else POOL_COLS, PAIR)
                     if n + 3 < PAIRS:
-                        turn(n + 3)
-                        square(n + 3, 0)
+                        turn(2 * n + 6)
+                        turn(2 * n + 7)
+                        square(2 * n + 6)
+                    if n + 4 < PAIRS:
+                        for g in range(SORT):
+                            part(2 * n + 8, g)
                 else:
                     if n + 2 < PAIRS:
                         quantize(n + 2, 0, 2)
                     if n + 3 < PAIRS:
-                        square(n + 3, 1)
+                        square(2 * n + 7)
+                        if n + 4 < PAIRS:
+                            for g in range(SORT):
+                                part(2 * n + 9, g)
                         weigh_pool(n + 3, POOL_COLS)

@@ -22,7 +22,7 @@ PASSES = K // (P * PACK)
 TILES = V // P
 PAIR = 2 * P
 PAIRS = V // PAIR
-POOL_COLS = 176
+POOL_COLS = 184
 WB = 1
 S1 = 128
 S2 = 176
@@ -37,6 +37,10 @@ QE = 1
 TL = 2
 WP = 2
 SORT = 0
+WA = 0
+WC = 0
+WD = 0
+WE = 3
 
 
 def tile_gated_heat_signature_s10_kernel(
@@ -122,24 +126,25 @@ def tile_gated_heat_signature_s10_kernel(
             words = phi_sb[i][:].bitcast(F32)
             for g in range(PASSES):
                 for u in range(2):
-                    if (i, g) in parted:
-                        nc.tensor.transpose(bank[:, g, u, :], parted[i, g][:, u, :], ident[:])
+                    if i in parted:
+                        nc.tensor.transpose(bank[:, g, u, :], parted[i][:, g, u, :], ident[:])
                     else:
                         nc.tensor.transpose(bank[:, g, u, :], words[:, 256 * g + u : 256 * (g + 1) : 2], ident[:])
 
-        def part(i, g):
-            parted[i, g] = work.tile([P, 2, P], F32, name="parted", bufs=4)
+        def part(i):
+            parted[i] = work.tile([P, PASSES, 2, P], F32, name="parted")
             words = phi_sb[i][:].bitcast(F32)
-            nc.scalar.copy(out=parted[i, g][:], in_=words[:, 256 * g : 256 * (g + 1)].rearrange("p (q u) -> p u q", u=2))
+            nc.scalar.copy(out=parted[i][:], in_=words.rearrange("p (g q u) -> p g u q", g=PASSES, u=2))
 
         def square(i):
-            sq = work.tile([P, P, PASSES * PACK], F32, name="sq", bufs=4)
+            sq = work.tile([P, PASSES, P, PACK], F32, name="sq", bufs=4)
             squares[i] = sq
-            nc.scalar.activation(
-                out=sq[:].rearrange("p v (w e) -> p v w e", e=2),
-                in_=turned[i][:].bitcast(BF16).rearrange("p g u (v e) -> p v (g u) e", e=2),
-                func=ACT.Square,
-            )
+            for g in range(PASSES):
+                nc.scalar.activation(
+                    out=sq[:, g, :, :].rearrange("p v (u e) -> p v u e", e=2),
+                    in_=turned[i][:, g, :, :].bitcast(BF16).rearrange("p u (v e) -> p v u e", e=2),
+                    func=ACT.Square,
+                )
 
         def weigh(n, lo, hi, engine, factor):
             if n not in weighted:
@@ -149,7 +154,7 @@ def tile_gated_heat_signature_s10_kernel(
                 if a < b:
                     engine.tensor_tensor(
                         out=weighted[n][:, j, :, a:b, :],
-                        in0=squares[2 * n + j][:, a:b, :].rearrange("p v (g t) -> p g v t", t=PACK),
+                        in0=squares[2 * n + j][:, :, a:b, :],
                         in1=factor[:, : PASSES * PACK]
                         .rearrange("p (g t) -> p g t", t=PACK)
                         .unsqueeze(2)
@@ -193,6 +198,20 @@ def tile_gated_heat_signature_s10_kernel(
                     stop=(g == PASSES - 1),
                 )
 
+        def warm(count):
+            if count:
+                bank = psum.tile([P, T], F32, name="acc", bufs=5)
+            for r in range(count):
+                nc.tensor.matmul_mx(
+                    out=bank[:],
+                    lhsT=heat_w[0][:, :P].bitcast(FP8X4),
+                    lhsT_scale=heat_s[0][:, :P],
+                    rhs=heat_w[0][:].bitcast(FP8X4),
+                    rhs_scale=heat_s[0][:],
+                    start=True,
+                    stop=True,
+                )
+
         def add_bias(i):
             logits[i] = work.tile([P, T], F32, name="logits")
             nc.vector.tensor_tensor(out=logits[i][:], in0=banks[i, "z"][:], in1=bias_row[:], op=ALU.add)
@@ -222,9 +241,9 @@ def tile_gated_heat_signature_s10_kernel(
 
         weavers = {"g": weave_heat_pool, "v": weave_heat, "a": weave_heat_scalar}
 
-        nc.vector.memset(gate_s[:].bitcast(I32), 0)
         nc.vector.memset(warm_in[:], 0.0)
         nc.vector.memset(c_f[:], 0.0)
+        nc.vector.memset(gate_s[:].bitcast(I32), 0)
         nc.vector.memset(resp_s[:].bitcast(I32), 0)
         nc.scalar.activation(out=warm_out[:], in_=warm_in[:], func=ACT.Sigmoid)
         make_identity(nc, ident[:])
@@ -281,6 +300,7 @@ def tile_gated_heat_signature_s10_kernel(
         if WP < 2:
             quantize_heat(1)
         weigh_pool(1, S1)
+        warm(WE)
         if TE:
             turn(4)
             turn(5)
@@ -324,15 +344,11 @@ def tile_gated_heat_signature_s10_kernel(
                         turn(2 * n + 6)
                         turn(2 * n + 7)
                         square(2 * n + 6)
-                    if n + 4 < PAIRS:
-                        for g in range(SORT):
-                            part(2 * n + 8, g)
                 else:
                     if n + 2 < PAIRS:
                         quantize(n + 2, 0, 2)
                     if n + 3 < PAIRS:
                         square(2 * n + 7)
-                        if n + 4 < PAIRS:
-                            for g in range(SORT):
-                                part(2 * n + 9, g)
                         weigh_pool(n + 3, POOL_COLS)
+                if i + 9 < TILES:
+                    part(i + 9)

@@ -22,25 +22,15 @@ PASSES = K // (P * PACK)
 TILES = V // P
 PAIR = 2 * P
 PAIRS = V // PAIR
-POOL_COLS = 184
-WB = 1
-S1 = 128
-S2 = 176
-W0 = "g"
-W1 = "a"
-TAILG = 1
-ZE = 1
-LO = "0a1b23g45r"
-BR = 0
-TE = 0
-QE = 1
-TL = 2
-WP = 2
-SORT = 0
-WA = 0
-WC = 0
-WD = 0
-WE = 3
+QUADRANTS = 4
+
+POOL_SHARE = 176
+TURN_BANKS = 2
+ACC_BANKS = 5
+FIRST_SORTED = 7
+SORT_AHEAD = 9
+WARM_PASSES = 3
+POOL_SUM_TILE = TILES - 3
 
 
 def tile_gated_heat_signature_s10_kernel(
@@ -50,19 +40,19 @@ def tile_gated_heat_signature_s10_kernel(
     with ExitStack() as ctx:
         keep = ctx.enter_context(tc.tile_pool(name="keep", bufs=1))
         work = ctx.enter_context(tc.tile_pool(name="work", bufs=3))
-        psum = ctx.enter_context(tc.psum_pool(name="psum", bufs=2))
+        psum = ctx.enter_context(tc.psum_pool(name="psum", bufs=1))
         ctx.enter_context(tc.manual_schedule())
 
         ident = keep.tile([P, P], F32, name="ident")
+        table_in = keep.tile([P, 1], F32, name="table_in")
+        table_out = keep.tile([P, 1], F32, name="table_out")
         c_bf = keep.tile([P, PASSES, PACK], BF16, name="c_bf")
-        c_f = keep.tile([P, P], F32, name="c_f")
-        c_rows = keep.tile([P, P], F32, name="c_rows")
-        c_ps = psum.tile([P, 2, P], F32, name="c_ps", bufs=1)
+        c_sb = keep.tile([P, P], F32, name="c_sb")
+        c_turned = keep.tile([P, P], F32, name="c_turned")
+        c_ps = psum.tile([P, 2, P], F32, name="c_ps")
         bias_bf = keep.tile([P, PACK], BF16, name="bias_bf")
-        bias_f = keep.tile([P, PACK], F32, name="bias_f")
+        bias_col = keep.tile([P, PACK], F32, name="bias_col")
         bias_row = keep.tile([P, T], F32, name="bias_row")
-        warm_in = keep.tile([P, 1], F32, name="warm_in")
-        warm_out = keep.tile([P, 1], F32, name="warm_out")
         gate_w = keep.tile([P, PASSES, 2 * T], U8, name="gate_w", align_bytes=64)
         gate_s = keep.tile([P, PASSES, T], U8, name="gate_s", align_bytes=64)
         resp_w = keep.tile([P, PASSES, T], U32, name="resp_w", align_bytes=64)
@@ -73,25 +63,29 @@ def tile_gated_heat_signature_s10_kernel(
         heat_s = [keep.tile([P, T], U8, name="heat_s%d" % g, align_bytes=64) for g in range(PASSES)]
         phi_sb = [keep.tile([P, K], BF16, name="phi%d" % i) for i in range(TILES)]
 
-        turned, squares, weighted, codes, scales = {}, {}, {}, {}, {}
-        banks, logits, gates, gated, parted = {}, {}, {}, {}, {}
+        sorted_words, turned, squares = {}, {}, {}
+        weighted, codes, scales = {}, {}, {}
+        banks, logits, gates, gated = {}, {}, {}, {}
+
+        def acc_bank(shape):
+            return psum.tile(shape, F32, name="acc", bufs=ACC_BANKS)
 
         def load_phi(i):
             nc.sync.dma_start(out=phi_sb[i][:], in_=phi[i * P : (i + 1) * P, :])
 
         def load_heat(g):
             rows = heat[g * P * PACK : (g + 1) * P * PACK, :]
-            nc.sync.dma_start(out=heat_raw[g][:], in_=rows.rearrange("(p j) n -> p j n", j=PACK))
+            nc.sync.dma_start(out=heat_raw[g][:], in_=rows.rearrange("(p t) n -> p t n", t=PACK))
 
-        def load_scales(plane, src):
-            for q in range(4):
+        def load_scales(tile, src):
+            for q in range(QUADRANTS):
                 nc.sync.dma_start(
-                    out=plane[32 * q : 32 * q + 4, :, :].bitcast(I32),
+                    out=tile[32 * q : 32 * q + 4, :, :].bitcast(I32),
                     in_=src[:, 4 * q : 4 * q + 4, :].rearrange("g r n -> r g n").bitcast(I32),
                 )
 
-        def weave_heat(g):
-            nc.vector.tensor_copy(
+        def interleave_heat(g, copy):
+            copy(
                 out=heat_bf[g][:].rearrange("p (n i) t -> p n t i", i=4),
                 in_=heat_raw[g][:].rearrange("p t (n i) -> p n t i", i=4),
             )
@@ -103,93 +97,75 @@ def tile_gated_heat_signature_s10_kernel(
                 in_=heat_bf[g][:].rearrange("p n t -> p (n t)"),
             )
 
-        def weave_heat_scalar(g):
-            nc.scalar.copy(
-                out=heat_bf[g][:].rearrange("p (n i) t -> p n t i", i=4),
-                in_=heat_raw[g][:].rearrange("p t (n i) -> p n t i", i=4),
-            )
+        def sort_words(i):
+            sorted_words[i] = work.tile([P, PASSES, 2, P], F32, name="sorted_words", bufs=4)
+            words = phi_sb[i][:].bitcast(F32)
+            nc.scalar.copy(out=sorted_words[i][:], in_=words.rearrange("v (g p u) -> v g u p", g=PASSES, u=2))
 
-        def weave_heat_pool(g):
-            for n0 in range(0, T, P):
-                nc.gpsimd.tensor_scalar(
-                    out=heat_bf[g][:, n0 : n0 + P, :],
-                    in0=heat_raw[g][:, :, n0 : n0 + P].rearrange("p t n -> p n t"),
-                    scalar1=1.0,
-                    scalar2=0.0,
-                    op0=ALU.mult,
-                    op1=ALU.add,
-                )
-
-        def turn(i, tag="turn", bufs=2):
-            bank = psum.tile([P, PASSES, 2, P], F32, name=tag, bufs=bufs)
+        def turn(i, bank):
             turned[i] = bank
             words = phi_sb[i][:].bitcast(F32)
             for g in range(PASSES):
                 for u in range(2):
-                    if i in parted:
-                        nc.tensor.transpose(bank[:, g, u, :], parted[i][:, g, u, :], ident[:])
+                    if i in sorted_words:
+                        columns = sorted_words[i][:, g, u, :]
                     else:
-                        nc.tensor.transpose(bank[:, g, u, :], words[:, 256 * g + u : 256 * (g + 1) : 2], ident[:])
+                        columns = words[:, 2 * P * g + u : 2 * P * (g + 1) : 2]
+                    nc.tensor.transpose(bank[:, g, u, :], columns, ident[:])
 
-        def part(i):
-            parted[i] = work.tile([P, PASSES, 2, P], F32, name="parted")
-            words = phi_sb[i][:].bitcast(F32)
-            nc.scalar.copy(out=parted[i][:], in_=words.rearrange("p (g q u) -> p g u q", g=PASSES, u=2))
+        def turn_bank():
+            return psum.tile([P, PASSES, 2, P], F32, name="turn", bufs=TURN_BANKS)
 
         def square(i):
-            sq = work.tile([P, PASSES, P, PACK], F32, name="sq", bufs=4)
-            squares[i] = sq
+            squares[i] = work.tile([P, PASSES, P, PACK], F32, name="squares", bufs=4)
             for g in range(PASSES):
                 nc.scalar.activation(
-                    out=sq[:, g, :, :].rearrange("p v (u e) -> p v u e", e=2),
+                    out=squares[i][:, g, :, :].rearrange("p v (u e) -> p v u e", e=2),
                     in_=turned[i][:, g, :, :].bitcast(BF16).rearrange("p u (v e) -> p v u e", e=2),
                     func=ACT.Square,
                 )
 
-        def weigh(n, lo, hi, engine, factor):
+        def weigh(n, lo, hi, engine, c_cols):
             if n not in weighted:
-                weighted[n] = work.tile([P, 2, PASSES, P, PACK], BF16, name="weighted", align_bytes=64, bufs=WB)
+                weighted[n] = work.tile([P, 2, PASSES, P, PACK], BF16, name="weighted", align_bytes=64, bufs=1)
+            factor = c_cols[:, : PASSES * PACK].rearrange("p (g t) -> p g t", t=PACK).unsqueeze(2)
             for j in range(2):
                 a, b = max(lo - j * P, 0), min(hi - j * P, P)
                 if a < b:
                     engine.tensor_tensor(
                         out=weighted[n][:, j, :, a:b, :],
                         in0=squares[2 * n + j][:, :, a:b, :],
-                        in1=factor[:, : PASSES * PACK]
-                        .rearrange("p (g t) -> p g t", t=PACK)
-                        .unsqueeze(2)
-                        .to_broadcast([P, PASSES, b - a, PACK]),
+                        in1=factor.to_broadcast([P, PASSES, b - a, PACK]),
                         op=ALU.mult,
                     )
 
         def weigh_pool(n, hi):
-            weigh(n, 0, hi, nc.gpsimd, c_f)
+            weigh(n, 0, hi, nc.gpsimd, c_sb)
 
-        def weigh_vector(n, lo, hi):
-            weigh(n, lo, hi, nc.vector, c_ps[:, 1, :])
+        def weigh_vector(n, lo):
+            weigh(n, lo, PAIR, nc.vector, c_ps[:, 1, :])
 
-        def quantize(n, j0, j1):
-            if n not in codes:
-                codes[n] = work.tile([P, 2, PASSES, P], U32, name="codes", align_bytes=64, bufs=4)
-                scales[n] = work.tile([P, 2, PASSES, P], U8, name="scales", align_bytes=64, bufs=4)
+        def quantize(n):
+            codes[n] = work.tile([P, 2, PASSES, P], U32, name="codes", align_bytes=64, bufs=4)
+            scales[n] = work.tile([P, 2, PASSES, P], U8, name="scales", align_bytes=64, bufs=4)
             nc.vector.quantize_mx(
-                out=codes[n][:, j0:j1, :, :].rearrange("p j g v -> p (j g v)").bitcast(FP8X4),
-                scales=scales[n][:, j0:j1, :, :].rearrange("p j g v -> p (j g v)"),
-                in_=weighted[n][:, j0:j1, :, :, :].rearrange("p j g v t -> p (j g v t)"),
+                out=codes[n][:].rearrange("p j g v -> p (j g v)").bitcast(FP8X4),
+                scales=scales[n][:].rearrange("p j g v -> p (j g v)"),
+                in_=weighted[n][:].rearrange("p j g v t -> p (j g v t)"),
             )
 
+        weights = {
+            "z": [(gate_w[:, g, :].bitcast(FP4X4), gate_s[:, g, :]) for g in range(PASSES)],
+            "h": [(heat_w[g][:].bitcast(FP8X4), heat_s[g][:]) for g in range(PASSES)],
+            "d": [(resp_w[:, g, :].bitcast(FP8X4), resp_s[:, g, :]) for g in range(PASSES)],
+        }
+
         def product(i, kind):
-            bank = psum.tile([P, T], F32, name="acc", bufs=5)
-            banks[i, kind] = bank
+            banks[i, kind] = acc_bank([P, T])
             n, j = divmod(i, 2)
-            for g in range(PASSES):
-                rhs, rhs_scale = {
-                    "z": (gate_w[:, g, :].bitcast(FP4X4), gate_s[:, g, :]),
-                    "h": (heat_w[g][:].bitcast(FP8X4), heat_s[g][:]),
-                    "d": (resp_w[:, g, :].bitcast(FP8X4), resp_s[:, g, :]),
-                }[kind]
+            for g, (rhs, rhs_scale) in enumerate(weights[kind]):
                 nc.tensor.matmul_mx(
-                    out=bank[:],
+                    out=banks[i, kind][:],
                     lhsT=codes[n][:, j, g, :].bitcast(FP8X4),
                     lhsT_scale=scales[n][:, j, g, :],
                     rhs=rhs,
@@ -198,16 +174,16 @@ def tile_gated_heat_signature_s10_kernel(
                     stop=(g == PASSES - 1),
                 )
 
-        def warm(count):
-            if count:
-                bank = psum.tile([P, T], F32, name="acc", bufs=5)
-            for r in range(count):
+        def warm_up():
+            bank = acc_bank([P, T])
+            rhs, rhs_scale = weights["h"][0]
+            for r in range(WARM_PASSES):
                 nc.tensor.matmul_mx(
                     out=bank[:],
                     lhsT=heat_w[0][:, :P].bitcast(FP8X4),
                     lhsT_scale=heat_s[0][:, :P],
-                    rhs=heat_w[0][:].bitcast(FP8X4),
-                    rhs_scale=heat_s[0][:],
+                    rhs=rhs,
+                    rhs_scale=rhs_scale,
                     start=True,
                     stop=True,
                 )
@@ -220,135 +196,114 @@ def tile_gated_heat_signature_s10_kernel(
             gates[i] = work.tile([P, T], F32, name="gates", bufs=5)
             nc.scalar.activation(out=gates[i][:], in_=logits[i][:], func=ACT.Sigmoid)
 
+        def make_gate(i):
+            product(i, "z")
+            add_bias(i)
+            sigmoid(i)
+
         def apply_gate(i):
             gated[i] = work.tile([P, T], F32, name="gated")
             nc.vector.tensor_tensor(out=gated[i][:], in0=banks[i, "h"][:], in1=gates[i][:], op=ALU.mult)
 
         def finish(i):
             result = work.tile([P, T], F32, name="result", bufs=4)
-            if TILES - TL - TAILG <= i < TILES - TL:
-                resp = work.tile([P, T], F32, name="resp")
-                nc.scalar.copy(out=resp[:], in_=banks[i, "d"][:])
-                nc.gpsimd.tensor_tensor(out=result[:], in0=resp[:], in1=gated[i][:], op=ALU.add)
+            if i == POOL_SUM_TILE:
+                response = work.tile([P, T], F32, name="response", bufs=1)
+                nc.scalar.copy(out=response[:], in_=banks[i, "d"][:])
+                nc.gpsimd.tensor_tensor(out=result[:], in0=response[:], in1=gated[i][:], op=ALU.add)
             else:
                 nc.vector.tensor_tensor(out=result[:], in0=banks[i, "d"][:], in1=gated[i][:], op=ALU.add)
             nc.sync.dma_start(out=out[i * P : (i + 1) * P, :], in_=result[:])
 
-        def gate_logits(i):
-            product(i, "z")
-            add_bias(i)
-            sigmoid(i)
-
-        weavers = {"g": weave_heat_pool, "v": weave_heat, "a": weave_heat_scalar}
-
-        nc.vector.memset(warm_in[:], 0.0)
-        nc.vector.memset(c_f[:], 0.0)
+        nc.vector.memset(table_in[:], 0.0)
+        nc.vector.memset(c_sb[:], 0.0)
         nc.vector.memset(gate_s[:].bitcast(I32), 0)
         nc.vector.memset(resp_s[:].bitcast(I32), 0)
-        nc.scalar.activation(out=warm_out[:], in_=warm_in[:], func=ACT.Sigmoid)
+        nc.scalar.activation(out=table_out[:], in_=table_in[:], func=ACT.Sigmoid)
         make_identity(nc, ident[:])
 
+        load_phi(0)
         nc.sync.dma_start(out=c_bf[:], in_=c.rearrange("(g p t) -> p g t", g=PASSES, t=PACK))
         nc.sync.dma_start(out=bias_bf[:], in_=bias.rearrange("(p j) -> p j", j=PACK))
-        for what in LO:
-            if what == "a":
-                load_heat(0)
-            elif what == "b":
-                load_heat(1)
-            elif what == "g":
-                nc.sync.dma_start(out=gate_w[:].bitcast(I32), in_=gate_words.rearrange("g p n -> p g n").bitcast(I32))
-                load_scales(gate_s, gate_scales)
-            elif what == "r":
-                load_scales(resp_s, resp_scales)
-                nc.sync.dma_start(out=resp_w[:].bitcast(I32), in_=resp_words.rearrange("g p n t -> p g (n t)").bitcast(I32))
-            else:
-                load_phi(int(what))
+        load_heat(0)
+        for i in range(1, 4):
+            load_phi(i)
+        load_heat(1)
+        nc.sync.dma_start(out=gate_w[:].bitcast(I32), in_=gate_words.rearrange("g p n -> p g n").bitcast(I32))
+        load_scales(gate_s, gate_scales)
+        load_phi(4)
+        load_phi(5)
+        load_scales(resp_s, resp_scales)
+        nc.sync.dma_start(out=resp_w[:].bitcast(I32), in_=resp_words.rearrange("g p n t -> p g (n t)").bitcast(I32))
         for i in range(6, TILES):
             load_phi(i)
 
-        nc.vector.tensor_copy(out=c_f[:, : PASSES * PACK], in_=c_bf[:].rearrange("p g t -> p (g t)"))
-        nc.vector.tensor_copy(out=bias_f[:], in_=bias_bf[:])
-        nc.tensor.transpose(c_ps[:, 0, :], c_f[:], ident[:])
-        nc.scalar.copy(out=c_rows[:], in_=c_ps[:, 0, :])
-        spread = psum.tile([P, PACK, P], F32, name="acc", bufs=5)
-        turn(0)
+        turn(0, turn_bank())
         square(0)
-        nc.tensor.transpose(c_ps[:, 1, :], c_rows[:], ident[:])
+
+        nc.vector.tensor_copy(out=c_sb[:, : PASSES * PACK], in_=c_bf[:].rearrange("p g t -> p (g t)"))
+        nc.vector.tensor_copy(out=bias_col[:], in_=bias_bf[:])
+        nc.tensor.transpose(c_ps[:, 0, :], c_sb[:], ident[:])
+        spread = acc_bank([P, PACK, P])
         for j in range(PACK):
-            nc.tensor.transpose(spread[:, j, :], bias_f[:, j : j + 1].to_broadcast([P, P]), ident[:])
-        if BR == 0:
-            nc.scalar.copy(out=bias_row[:].rearrange("p (n j) -> p n j", j=PACK), in_=spread[:].rearrange("p j n -> p n j"))
-        turn(1)
+            nc.tensor.transpose(spread[:, j, :], bias_col[:, j : j + 1].to_broadcast([P, P]), ident[:])
+        nc.scalar.copy(out=c_turned[:], in_=c_ps[:, 0, :])
+        nc.scalar.copy(out=bias_row[:].rearrange("p (n j) -> p n j", j=PACK), in_=spread[:].rearrange("p j n -> p n j"))
+        turn(1, turn_bank())
+        nc.tensor.transpose(c_ps[:, 1, :], c_turned[:], ident[:])
         square(1)
-        weave_heat(0)
-        weigh_vector(0, 0, P)
+
+        interleave_heat(0, nc.vector.tensor_copy)
+        weigh(0, 0, P, nc.vector, c_sb)
         quantize_heat(0)
-        if WP == 0:
-            weavers[W1](1)
-        turn(2, "acc", 5)
-        turn(3, "acc", 5)
+        turn(2, acc_bank([P, PASSES, 2, P]))
+        turn(3, acc_bank([P, PASSES, 2, P]))
         square(2)
-        if WP == 1:
-            weavers[W1](1)
         square(3)
-        if WP == 2:
-            weavers[W1](1)
-        if BR == 1:
-            nc.scalar.copy(out=bias_row[:].rearrange("p (n j) -> p n j", j=PACK), in_=spread[:].rearrange("p j n -> p n j"))
-        weigh_vector(0, P, PAIR)
-        quantize(0, 0, 2)
-        if WP < 2:
-            quantize_heat(1)
-        weigh_pool(1, S1)
-        warm(WE)
-        if TE:
-            turn(4)
-            turn(5)
+        interleave_heat(1, nc.scalar.copy)
+        weigh_vector(0, P)
+        quantize(0)
+        weigh_pool(1, P)
+        warm_up()
         product(0, "z")
-        if not TE:
-            turn(4)
-            turn(5)
-        weigh_vector(1, S1, PAIR)
+        turn(4, turn_bank())
+        turn(5, turn_bank())
+        weigh_vector(1, P)
         add_bias(0)
-        if WP == 2:
-            quantize_heat(1)
+        quantize_heat(1)
         square(4)
         sigmoid(0)
         square(5)
-        if ZE == 2:
-            gate_logits(1)
-        if QE:
-            quantize(1, 0, 2)
-            weigh_pool(2, S2)
+        quantize(1)
+        weigh_pool(2, POOL_SHARE)
+        for i in range(FIRST_SORTED, SORT_AHEAD):
+            sort_words(i)
 
-        done = ZE
-        for n in range(PAIRS):
-            for i in (2 * n, 2 * n + 1):
-                product(i, "h")
-                apply_gate(i)
-                if done == i + 1 < TILES:
-                    gate_logits(done)
-                    done = done + 1
-                product(i, "d")
-                finish(i)
-                if i >= TILES - 4 and done < TILES:
-                    gate_logits(done)
-                    done = done + 1
-                if i % 2 == 0:
-                    if i == 0 and not QE:
-                        quantize(1, 0, 2)
-                        weigh_pool(2, S2)
-                    if n + 2 < PAIRS:
-                        weigh_vector(n + 2, S2 if i == 0 else POOL_COLS, PAIR)
-                    if n + 3 < PAIRS:
-                        turn(2 * n + 6)
-                        turn(2 * n + 7)
-                        square(2 * n + 6)
-                else:
-                    if n + 2 < PAIRS:
-                        quantize(n + 2, 0, 2)
-                    if n + 3 < PAIRS:
-                        square(2 * n + 7)
-                        weigh_pool(n + 3, POOL_COLS)
-                if i + 9 < TILES:
-                    part(i + 9)
+        next_gate = 1
+        for i in range(TILES):
+            n, j = divmod(i, 2)
+            product(i, "h")
+            apply_gate(i)
+            if next_gate == i + 1 < TILES:
+                make_gate(next_gate)
+                next_gate = next_gate + 1
+            product(i, "d")
+            finish(i)
+            if n >= PAIRS - 2 and next_gate < TILES:
+                make_gate(next_gate)
+                next_gate = next_gate + 1
+            if j == 0:
+                if n + 2 < PAIRS:
+                    weigh_vector(n + 2, POOL_SHARE)
+                if n + 3 < PAIRS:
+                    turn(2 * (n + 3), turn_bank())
+                    turn(2 * (n + 3) + 1, turn_bank())
+                    square(2 * (n + 3))
+            else:
+                if n + 2 < PAIRS:
+                    quantize(n + 2)
+                if n + 3 < PAIRS:
+                    square(2 * (n + 3) + 1)
+                    weigh_pool(n + 3, POOL_SHARE)
+            if i + SORT_AHEAD < TILES:
+                sort_words(i + SORT_AHEAD)

from contextlib import ExitStack

import concourse.mybir as mybir
from concourse.masks import make_identity

V, K, T = 2560, 1024, 512
FLOPS = 3 * 2 * V * K * T

F32 = mybir.dt.float32
BF16 = mybir.dt.bfloat16
I32 = mybir.dt.int32
U32 = mybir.dt.uint32
U8 = mybir.dt.uint8
FP8X4 = mybir.dt.float8_e4m3fn_x4
FP4X4 = mybir.dt.float4_e2m1fn_x4
ACT = mybir.ActivationFunctionType
ALU = mybir.AluOpType

P = 128
PACK = 4
PASSES = K // (P * PACK)
TILES = V // P
PAIR = 2 * P
PAIRS = V // PAIR
QUADRANTS = 4

POOL_SHARE = 176
TURN_BANKS = 2
ACC_BANKS = 5
FIRST_SORTED = 7
SORT_AHEAD = 9
WARM_PASSES = 3
POOL_SUM_TILE = TILES - 3


def tile_gated_heat_signature_s10_kernel(
    tc, phi, c, heat, gate_words, gate_scales, resp_words, resp_scales, bias, out
):
    nc = tc.nc
    with ExitStack() as ctx:
        keep = ctx.enter_context(tc.tile_pool(name="keep", bufs=1))
        work = ctx.enter_context(tc.tile_pool(name="work", bufs=3))
        psum = ctx.enter_context(tc.psum_pool(name="psum", bufs=1))
        ctx.enter_context(tc.manual_schedule())

        ident = keep.tile([P, P], F32, name="ident")
        table_in = keep.tile([P, 1], F32, name="table_in")
        table_out = keep.tile([P, 1], F32, name="table_out")
        c_bf = keep.tile([P, PASSES, PACK], BF16, name="c_bf")
        c_sb = keep.tile([P, P], F32, name="c_sb")
        c_turned = keep.tile([P, P], F32, name="c_turned")
        c_ps = psum.tile([P, 2, P], F32, name="c_ps")
        bias_bf = keep.tile([P, PACK], BF16, name="bias_bf")
        bias_col = keep.tile([P, PACK], F32, name="bias_col")
        bias_row = keep.tile([P, T], F32, name="bias_row")
        gate_w = keep.tile([P, PASSES, 2 * T], U8, name="gate_w", align_bytes=64)
        gate_s = keep.tile([P, PASSES, T], U8, name="gate_s", align_bytes=64)
        resp_w = keep.tile([P, PASSES, T], U32, name="resp_w", align_bytes=64)
        resp_s = keep.tile([P, PASSES, T], U8, name="resp_s", align_bytes=64)
        heat_raw = [keep.tile([P, PACK, T], BF16, name="heat_raw%d" % g) for g in range(PASSES)]
        heat_bf = [keep.tile([P, T, PACK], BF16, name="heat_bf%d" % g, align_bytes=64) for g in range(PASSES)]
        heat_w = [keep.tile([P, T], U32, name="heat_w%d" % g, align_bytes=64) for g in range(PASSES)]
        heat_s = [keep.tile([P, T], U8, name="heat_s%d" % g, align_bytes=64) for g in range(PASSES)]
        phi_sb = [keep.tile([P, K], BF16, name="phi%d" % i) for i in range(TILES)]

        sorted_words, turned, squares = {}, {}, {}
        weighted, codes, scales = {}, {}, {}
        banks, logits, gates, gated = {}, {}, {}, {}

        def acc_bank(shape):
            return psum.tile(shape, F32, name="acc", bufs=ACC_BANKS)

        def load_phi(i):
            nc.sync.dma_start(out=phi_sb[i][:], in_=phi[i * P : (i + 1) * P, :])

        def load_heat(g):
            rows = heat[g * P * PACK : (g + 1) * P * PACK, :]
            nc.sync.dma_start(out=heat_raw[g][:], in_=rows.rearrange("(p t) n -> p t n", t=PACK))

        def load_scales(tile, src):
            for q in range(QUADRANTS):
                nc.sync.dma_start(
                    out=tile[32 * q : 32 * q + 4, :, :].bitcast(I32),
                    in_=src[:, 4 * q : 4 * q + 4, :].rearrange("g r n -> r g n").bitcast(I32),
                )

        def interleave_heat(g, copy):
            copy(
                out=heat_bf[g][:].rearrange("p (n i) t -> p n t i", i=4),
                in_=heat_raw[g][:].rearrange("p t (n i) -> p n t i", i=4),
            )

        def quantize_heat(g):
            nc.vector.quantize_mx(
                out=heat_w[g][:].bitcast(FP8X4),
                scales=heat_s[g][:],
                in_=heat_bf[g][:].rearrange("p n t -> p (n t)"),
            )

        def sort_words(i):
            sorted_words[i] = work.tile([P, PASSES, 2, P], F32, name="sorted_words", bufs=4)
            words = phi_sb[i][:].bitcast(F32)
            nc.scalar.copy(out=sorted_words[i][:], in_=words.rearrange("v (g p u) -> v g u p", g=PASSES, u=2))

        def turn(i, bank):
            turned[i] = bank
            words = phi_sb[i][:].bitcast(F32)
            for g in range(PASSES):
                for u in range(2):
                    if i in sorted_words:
                        columns = sorted_words[i][:, g, u, :]
                    else:
                        columns = words[:, 2 * P * g + u : 2 * P * (g + 1) : 2]
                    nc.tensor.transpose(bank[:, g, u, :], columns, ident[:])

        def turn_bank():
            return psum.tile([P, PASSES, 2, P], F32, name="turn", bufs=TURN_BANKS)

        def square(i):
            squares[i] = work.tile([P, PASSES, P, PACK], F32, name="squares", bufs=4)
            for g in range(PASSES):
                nc.scalar.activation(
                    out=squares[i][:, g, :, :].rearrange("p v (u e) -> p v u e", e=2),
                    in_=turned[i][:, g, :, :].bitcast(BF16).rearrange("p u (v e) -> p v u e", e=2),
                    func=ACT.Square,
                )

        def weigh(n, lo, hi, engine, c_cols):
            if n not in weighted:
                weighted[n] = work.tile([P, 2, PASSES, P, PACK], BF16, name="weighted", align_bytes=64, bufs=1)
            factor = c_cols[:, : PASSES * PACK].rearrange("p (g t) -> p g t", t=PACK).unsqueeze(2)
            for j in range(2):
                a, b = max(lo - j * P, 0), min(hi - j * P, P)
                if a < b:
                    engine.tensor_tensor(
                        out=weighted[n][:, j, :, a:b, :],
                        in0=squares[2 * n + j][:, :, a:b, :],
                        in1=factor.to_broadcast([P, PASSES, b - a, PACK]),
                        op=ALU.mult,
                    )

        def weigh_pool(n, hi):
            weigh(n, 0, hi, nc.gpsimd, c_sb)

        def weigh_vector(n, lo):
            weigh(n, lo, PAIR, nc.vector, c_ps[:, 1, :])

        def quantize(n):
            codes[n] = work.tile([P, 2, PASSES, P], U32, name="codes", align_bytes=64, bufs=4)
            scales[n] = work.tile([P, 2, PASSES, P], U8, name="scales", align_bytes=64, bufs=4)
            nc.vector.quantize_mx(
                out=codes[n][:].rearrange("p j g v -> p (j g v)").bitcast(FP8X4),
                scales=scales[n][:].rearrange("p j g v -> p (j g v)"),
                in_=weighted[n][:].rearrange("p j g v t -> p (j g v t)"),
            )

        weights = {
            "z": [(gate_w[:, g, :].bitcast(FP4X4), gate_s[:, g, :]) for g in range(PASSES)],
            "h": [(heat_w[g][:].bitcast(FP8X4), heat_s[g][:]) for g in range(PASSES)],
            "d": [(resp_w[:, g, :].bitcast(FP8X4), resp_s[:, g, :]) for g in range(PASSES)],
        }

        def product(i, kind):
            banks[i, kind] = acc_bank([P, T])
            n, j = divmod(i, 2)
            for g, (rhs, rhs_scale) in enumerate(weights[kind]):
                nc.tensor.matmul_mx(
                    out=banks[i, kind][:],
                    lhsT=codes[n][:, j, g, :].bitcast(FP8X4),
                    lhsT_scale=scales[n][:, j, g, :],
                    rhs=rhs,
                    rhs_scale=rhs_scale,
                    start=(g == 0),
                    stop=(g == PASSES - 1),
                )

        def warm_up():
            bank = acc_bank([P, T])
            rhs, rhs_scale = weights["h"][0]
            for r in range(WARM_PASSES):
                nc.tensor.matmul_mx(
                    out=bank[:],
                    lhsT=heat_w[0][:, :P].bitcast(FP8X4),
                    lhsT_scale=heat_s[0][:, :P],
                    rhs=rhs,
                    rhs_scale=rhs_scale,
                    start=True,
                    stop=True,
                )

        def add_bias(i):
            logits[i] = work.tile([P, T], F32, name="logits")
            nc.vector.tensor_tensor(out=logits[i][:], in0=banks[i, "z"][:], in1=bias_row[:], op=ALU.add)

        def sigmoid(i):
            gates[i] = work.tile([P, T], F32, name="gates", bufs=5)
            nc.scalar.activation(out=gates[i][:], in_=logits[i][:], func=ACT.Sigmoid)

        def make_gate(i):
            product(i, "z")
            add_bias(i)
            sigmoid(i)

        def apply_gate(i):
            gated[i] = work.tile([P, T], F32, name="gated")
            nc.vector.tensor_tensor(out=gated[i][:], in0=banks[i, "h"][:], in1=gates[i][:], op=ALU.mult)

        def finish(i):
            result = work.tile([P, T], F32, name="result", bufs=4)
            if i == POOL_SUM_TILE:
                response = work.tile([P, T], F32, name="response", bufs=1)
                nc.scalar.copy(out=response[:], in_=banks[i, "d"][:])
                nc.gpsimd.tensor_tensor(out=result[:], in0=response[:], in1=gated[i][:], op=ALU.add)
            else:
                nc.vector.tensor_tensor(out=result[:], in0=banks[i, "d"][:], in1=gated[i][:], op=ALU.add)
            nc.sync.dma_start(out=out[i * P : (i + 1) * P, :], in_=result[:])

        nc.vector.memset(table_in[:], 0.0)
        nc.vector.memset(c_sb[:], 0.0)
        nc.vector.memset(gate_s[:].bitcast(I32), 0)
        nc.vector.memset(resp_s[:].bitcast(I32), 0)
        nc.scalar.activation(out=table_out[:], in_=table_in[:], func=ACT.Sigmoid)
        make_identity(nc, ident[:])

        load_phi(0)
        nc.sync.dma_start(out=c_bf[:], in_=c.rearrange("(g p t) -> p g t", g=PASSES, t=PACK))
        nc.sync.dma_start(out=bias_bf[:], in_=bias.rearrange("(p j) -> p j", j=PACK))
        load_heat(0)
        for i in range(1, 4):
            load_phi(i)
        load_heat(1)
        nc.sync.dma_start(out=gate_w[:].bitcast(I32), in_=gate_words.rearrange("g p n -> p g n").bitcast(I32))
        load_scales(gate_s, gate_scales)
        load_phi(4)
        load_phi(5)
        load_scales(resp_s, resp_scales)
        nc.sync.dma_start(out=resp_w[:].bitcast(I32), in_=resp_words.rearrange("g p n t -> p g (n t)").bitcast(I32))
        for i in range(6, TILES):
            load_phi(i)

        turn(0, turn_bank())
        square(0)

        nc.vector.tensor_copy(out=c_sb[:, : PASSES * PACK], in_=c_bf[:].rearrange("p g t -> p (g t)"))
        nc.vector.tensor_copy(out=bias_col[:], in_=bias_bf[:])
        nc.tensor.transpose(c_ps[:, 0, :], c_sb[:], ident[:])
        spread = acc_bank([P, PACK, P])
        for j in range(PACK):
            nc.tensor.transpose(spread[:, j, :], bias_col[:, j : j + 1].to_broadcast([P, P]), ident[:])
        nc.scalar.copy(out=c_turned[:], in_=c_ps[:, 0, :])
        nc.scalar.copy(out=bias_row[:].rearrange("p (n j) -> p n j", j=PACK), in_=spread[:].rearrange("p j n -> p n j"))
        turn(1, turn_bank())
        nc.tensor.transpose(c_ps[:, 1, :], c_turned[:], ident[:])
        square(1)

        interleave_heat(0, nc.vector.tensor_copy)
        weigh(0, 0, P, nc.vector, c_sb)
        quantize_heat(0)
        turn(2, acc_bank([P, PASSES, 2, P]))
        turn(3, acc_bank([P, PASSES, 2, P]))
        square(2)
        square(3)
        interleave_heat(1, nc.scalar.copy)
        weigh_vector(0, P)
        quantize(0)
        weigh_pool(1, P)
        warm_up()
        product(0, "z")
        turn(4, turn_bank())
        turn(5, turn_bank())
        weigh_vector(1, P)
        add_bias(0)
        quantize_heat(1)
        square(4)
        sigmoid(0)
        square(5)
        quantize(1)
        weigh_pool(2, POOL_SHARE)
        for i in range(FIRST_SORTED, SORT_AHEAD):
            sort_words(i)

        next_gate = 1
        for i in range(TILES):
            n, j = divmod(i, 2)
            product(i, "h")
            apply_gate(i)
            if next_gate == i + 1 < TILES:
                make_gate(next_gate)
                next_gate = next_gate + 1
            product(i, "d")
            finish(i)
            if n >= PAIRS - 2 and next_gate < TILES:
                make_gate(next_gate)
                next_gate = next_gate + 1
            if j == 0:
                if n + 2 < PAIRS:
                    weigh_vector(n + 2, POOL_SHARE)
                if n + 3 < PAIRS:
                    turn(2 * (n + 3), turn_bank())
                    turn(2 * (n + 3) + 1, turn_bank())
                    square(2 * (n + 3))
            else:
                if n + 2 < PAIRS:
                    quantize(n + 2)
                if n + 3 < PAIRS:
                    square(2 * (n + 3) + 1)
                    weigh_pool(n + 3, POOL_SHARE)
            if i + SORT_AHEAD < TILES:
                sort_words(i + SORT_AHEAD)
